import numpy as np
import ml_dtypes


def mxq(x, axis, fmt="e4m3"):
    dtype, down = {"e4m3": (ml_dtypes.float8_e4m3fn, 7), "e5m2": (ml_dtypes.float8_e5m2, 14)}[fmt]
    v = np.moveaxis(np.asarray(x, np.float32).astype(ml_dtypes.bfloat16).astype(np.float64), axis, -1)
    blocks = v.reshape(v.shape[:-1] + (-1, 32))
    amax = np.abs(blocks).max(-1, keepdims=True)
    byte = np.maximum(np.where(amax > 0, np.frexp(amax)[1] - 1 + 127, 0) - down, 1)
    scale = np.exp2(byte - 127.0)
    codes = (blocks / scale).astype(np.float32).astype(dtype).astype(np.float64)
    return np.moveaxis((codes * scale).reshape(v.shape), -1, axis)


WIDE = False


def mx_kscale(k):
    if not WIDE:
        return np.ones(k)
    levels = np.array([10, -10, 5, -5, 0])
    if k % 512:
        return np.exp2(np.random.permutation(np.resize(levels, k // 32))).repeat(32)
    a = np.empty((k // 512, 16))
    for p in range(k // 512):
        a[p, :8] = np.random.permutation(np.resize(levels, 8))
        for g in range(8):
            far = levels[np.abs(levels - a[p, g]) >= 10]
            a[p, g + 8] = far[np.random.randint(len(far))]
    return np.exp2(a.ravel()).repeat(32)


def f64(x):
    return np.asarray(x).astype(np.float64)


def striped(idx):
    return np.tile(np.asarray(idx).reshape(-1, 16).T, (8, 1)).astype(np.uint16)


def unstriped(offs):
    return offs[:16].T.reshape(-1).astype(np.int64)


E2M1 = np.array([0.0, 0.5, 1.0, 1.5, 2.0, 3.0, 4.0, 6.0, -0.0, -0.5, -1.0, -1.5, -2.0, -3.0, -4.0, -6.0])


def pack_weight(w, fmt):
    k, n = w.shape
    w = f64(np.asarray(w, np.float32).astype(ml_dtypes.bfloat16)).reshape(k // 32, 32, n)
    amax = np.abs(w).max(1)
    if fmt == "e4m3":
        byte = np.frexp(amax)[1] - 1 + 127 - 7
    else:
        mant, ex = np.frexp(amax / 6.0)
        byte = np.where(mant > 0.5, ex, ex - 1) + 127
    byte = np.clip(np.where(amax > 0, byte, 1), 1, 254)
    scaled = (w * np.exp2(127.0 - byte)[:, None, :]).reshape(k, n).astype(np.float32)
    by_word = np.ascontiguousarray(scaled.reshape(k // 512, 128, 4, n).transpose(0, 1, 3, 2))
    if fmt == "e4m3":
        words = by_word.astype(ml_dtypes.float8_e4m3fn).view(np.uint8)
    else:
        c = by_word.astype(ml_dtypes.float4_e2m1fn).view(np.uint8) & 0xF
        words = (c[..., 0::2] | (c[..., 1::2] << 4)).reshape(k // 512, 128, 2 * n)
    return np.ascontiguousarray(words), np.ascontiguousarray(byte.astype(np.uint8).reshape(k // 512, 16, n))


def unpack_weight(words, scales, fmt):
    g, _, n = scales.shape
    words = np.ascontiguousarray(words).reshape(g, 128, n, -1)
    if fmt == "e4m3":
        vals = words.view(ml_dtypes.float8_e4m3fn).astype(np.float64)
    else:
        nib = np.empty((g, 128, n, 4), np.uint8)
        nib[..., 0::2] = words & 0xF
        nib[..., 1::2] = words >> 4
        vals = E2M1[nib]
    vals = vals * np.repeat(np.exp2(scales.astype(np.float64) - 127.0), 8, axis=1)[..., None]
    return vals.transpose(0, 1, 3, 2).reshape(g * 512, n)


D, T, I, Q, E, U = 512, 2048, 512, 128, 512, 256


def setup_inputs():
    n = np.random.standard_normal
    idx = np.random.permutation(T)[:I]
    idx2 = np.repeat(np.random.permutation(U)[:I // 16], 16)
    fd = mx_kscale(D)
    fi = mx_kscale(I)
    ti = np.ones(T)
    ti[idx] = fi
    keysp = pack_weight(n((D, T)) / fd[:, None], "e4m3")
    return {
        "query": (n((D, Q)) * 0.4 / np.sqrt(D) * fd[:, None]).astype(np.float32),
        "keys_words": keysp[0],
        "keys_scales": keysp[1],
        "kscale": np.tile(np.random.uniform(0.4, 2.0, U), (128, 1)).astype(np.float32),
        "vscale": np.tile(np.random.uniform(0.4, 2.0, U), (128, 1)).astype(np.float32),
        "size": (np.random.uniform(0.5, 2.0, (1, I)) * fi).astype(np.float32),
        "vals": (n((E, T)) / ti).astype(np.float32),
        "offs": striped(idx),
        "offs2": striped(idx2),
    }


def reference(query, keys_words, keys_scales, kscale, vscale, size, vals, offs, offs2):
    idx = unstriped(offs)
    idx2 = unstriped(offs2)
    keysu = unpack_weight(keys_words, keys_scales, "e4m3")
    queryq = mxq(f64(query), 0, "e4m3")
    keysidxg = keysu[:, idx]
    a = queryq.T @ keysidxg
    s = a * f64(kscale)[:1][:, idx2]
    p = np.exp(s - np.max(s, axis=1, keepdims=True))
    w = p * f64(vscale)[:1][:, idx2] * f64(size) / np.sum(p, axis=1, keepdims=True)
    wt = w.T
    vt = f64(vals)[:, idx].T
    wtq = mxq(wt, 0, "e4m3")
    vtq = mxq(vt, 0, "e4m3")
    o = wtq.T @ vtq
    return o

@@ -1,0 +1,141 @@
+from contextlib import ExitStack
+
+import concourse.mybir as mybir
+from concourse.masks import make_identity
+
+F32 = mybir.dt.float32
+BF16 = mybir.dt.bfloat16
+I32 = mybir.dt.int32
+U32 = mybir.dt.uint32
+U16 = mybir.dt.uint16
+U8 = mybir.dt.uint8
+FP8X4 = mybir.dt.float8_e4m3fn_x4
+ALU = mybir.AluOpType
+ACT = mybir.ActivationFunctionType
+
+P = 128
+D, T, I, Q, E, U = 512, 2048, 512, 128, 512, 256
+PACK = 4
+PAGE_WINDOW = 544
+FLOPS = 2 * D * Q * I + 2 * I * Q * E
+
+
+def tile_attend_pagescales_kernel(tc, query, keys_words, keys_scales, kscale, vscale, size, vals, offs, offs2, out):
+    nc = tc.nc
+    with ExitStack() as ctx:
+        sb = ctx.enter_context(tc.tile_pool(name="sb", bufs=1))
+        ps = ctx.enter_context(tc.psum_pool(name="ps", bufs=1))
+        ps2 = ctx.enter_context(tc.psum_pool(name="ps2", bufs=2))
+
+        token_list = sb.tile([P, I // 16], U16, name="token_list")
+        page_list = sb.tile([P, I // 16], U16, name="page_list")
+        key_pool = sb.tile([P, T], I32, name="key_pool")
+        key_scale_pool = sb.tile([P, T], U8, name="key_scale_pool")
+        q_raw = sb.tile([P, PACK, Q], F32, name="q_raw")
+        ks_pool = sb.tile([P, PAGE_WINDOW], F32, name="ks_pool")
+        vs_pool = sb.tile([P, PAGE_WINDOW], F32, name="vs_pool")
+        size_col = sb.tile([P, PACK], F32, name="size_col")
+        val_pool = [sb.tile([P, T], F32, name="val_pool%d" % j, tag="val_pool%d" % j, align_bytes=64) for j in range(E // P)]
+        ident = sb.tile([P, P], F32, name="ident")
+
+        nc.gpsimd.memset(key_scale_pool[:].bitcast(I32), 0)
+        nc.vector.memset(ks_pool[:, U:], 0.0)
+        nc.vector.memset(vs_pool[:, U:], 0.0)
+        make_identity(nc, ident[:])
+
+        nc.sync.dma_start(token_list[:], offs)
+        nc.sync.dma_start(size_col[:], size.rearrange("o (p t) -> (o p) t", t=PACK))
+        for quad in range(4):
+            nc.sync.dma_start(
+                key_scale_pool[32 * quad : 32 * quad + 4, :].bitcast(I32),
+                keys_scales[0, 4 * quad : 4 * quad + 4, :].bitcast(I32),
+            )
+        nc.sync.dma_start(q_raw[:], query.rearrange("(p j) q -> p j q", j=PACK))
+        nc.sync.dma_start(key_pool[:], keys_words[0].rearrange("p n t -> p (n t)").bitcast(I32))
+        nc.sync.dma_start(page_list[:], offs2)
+        nc.sync.dma_start(vs_pool[:, :U], vscale)
+        nc.sync.dma_start(ks_pool[:, :U], kscale)
+        for j in range(E // P):
+            nc.sync.dma_start(val_pool[j][:], vals[j * P : (j + 1) * P, :])
+
+        def quantise(name, grouped, width, codes_tag):
+            codes = sb.tile([P, width], U32, name=name + "_codes", tag=codes_tag, align_bytes=64)
+            scales = sb.tile([P, width], U8, name=name + "_scales", align_bytes=64)
+            nc.vector.quantize_mx(out=codes[:].bitcast(FP8X4), scales=scales[:], in_=grouped[:])
+            return codes, scales
+
+        def turn(rows_bf16, grouped):
+            words = rows_bf16[:].bitcast(F32)
+            turned = ps2.tile([P, 2, P], F32, name="turned")
+            for u in range(2):
+                nc.tensor.transpose(turned[:, u, :], words[:, u : I // 2 : 2], ident[:])
+            nc.scalar.copy(
+                grouped.bitcast(F32).rearrange("p (r u) -> p r u", u=2),
+                turned[:].rearrange("p u r -> p r u"),
+            )
+
+        key_scales = sb.tile([P, I], U8, name="key_scales", align_bytes=64)
+        nc.vector.tensor_copy(key_scales[:], key_scale_pool[:].indirect(token_list[:]))
+        q_grouped = sb.tile([P, PACK * Q], BF16, name="q_grouped", align_bytes=64)
+        nc.scalar.copy(q_grouped[:].rearrange("p (q j) -> p q j", j=PACK), q_raw[:].rearrange("p j q -> p q j"))
+        q_codes, q_scales = quantise("q", q_grouped, Q, "q_codes")
+        key_codes = sb.tile([P, I], U32, name="key_codes", align_bytes=64)
+        nc.vector.tensor_copy(key_codes[:], key_pool[:].bitcast(U32).indirect(token_list[:]))
+
+        a_ps = ps.tile([P, I], F32, name="a_ps")
+        nc.tensor.matmul_mx(
+            out=a_ps[:], lhsT=q_codes[:].bitcast(FP8X4), lhsT_scale=q_scales[:],
+            rhs=key_codes[:].bitcast(FP8X4), rhs_scale=key_scales[:], start=True, stop=True,
+        )
+        a_sb = sb.tile([P, I], F32, name="a_sb")
+        nc.scalar.copy(a_sb[:], a_ps[:])
+
+        size_ps = ps.tile([P, PACK, P], F32, name="size_ps")
+        for t in range(PACK):
+            nc.tensor.transpose(size_ps[:, t, :], size_col[:, t : t + 1].to_broadcast([P, P]), ident[:])
+        size_rows = sb.tile([P, I], F32, name="size_rows")
+        nc.scalar.copy(size_rows[:].rearrange("q (p t) -> q p t", t=PACK), size_ps[:].rearrange("q t p -> q p t"))
+        factor = sb.tile([P, I], F32, name="factor")
+        nc.vector.tensor_tensor(factor[:], vs_pool[:].indirect(page_list[:]), size_rows[:], ALU.mult)
+
+        s = sb.tile([P, I], F32, name="s")
+        nc.vector.tensor_tensor(s[:], ks_pool[:].indirect(page_list[:]), a_sb[:], ALU.mult)
+        neg_max = sb.tile([P, 1], F32, name="neg_max")
+        nc.vector.tensor_reduce(neg_max[:], s[:], mybir.AxisListType.X, ALU.max, negate=True)
+        prob = sb.tile([P, I], F32, name="prob")
+        row_sum = sb.tile([P, 1], F32, name="row_sum")
+        nc.scalar.activation(prob[:], s[:], ACT.Exp, bias=neg_max[:], scale=1.0, accum_out=row_sum[:])
+
+        def gather_values(j, grouped):
+            picked = sb.tile([P, I], BF16, name="picked%d" % j, align_bytes=64)
+            nc.vector.tensor_copy(picked[:], val_pool[j][:].indirect(token_list[:]))
+            turn(picked, grouped)
+
+        def multiply(j, v_codes, v_scales):
+            o_ps = ps2.tile([P, P], F32, name="o_ps")
+            nc.tensor.matmul_mx(
+                out=o_ps[:], lhsT=first_codes[:, :Q].bitcast(FP8X4), lhsT_scale=first_scales[:, :Q],
+                rhs=v_codes.bitcast(FP8X4), rhs_scale=v_scales, start=True, stop=True,
+            )
+            o_sb = sb.tile([P, P], F32, name="o_sb%d" % j)
+            nc.scalar.copy(o_sb[:], o_ps[:])
+            nc.sync.dma_start(out[:, j * P : (j + 1) * P], o_sb[:])
+
+        first_grouped = sb.tile([P, PACK * (Q + P)], BF16, name="first_grouped", align_bytes=64)
+        gather_values(0, first_grouped[:, PACK * Q :])
+
+        inv_sum = sb.tile([P, 1], F32, name="inv_sum")
+        nc.vector.reciprocal(inv_sum[:], row_sum[:])
+        w = sb.tile([P, I], BF16, name="w", align_bytes=64)
+        nc.vector.scalar_tensor_tensor(w[:], prob[:], inv_sum[:], factor[:], ALU.mult, ALU.mult)
+        turn(w, first_grouped[:, : PACK * Q])
+
+        grouped = [sb.tile([P, PACK * P], BF16, name="grouped%d" % j, align_bytes=64) for j in range(1, E // P)]
+        gather_values(1, grouped[0][:])
+        first_codes, first_scales = quantise("first", first_grouped, Q + P, "val_pool1")
+        multiply(0, first_codes[:, Q:], first_scales[:, Q:])
+        for j in range(1, E // P):
+            if j + 1 < E // P:
+                gather_values(j + 1, grouped[j][:])
+            v_codes, v_scales = quantise("v%d" % j, grouped[j - 1], P, "val_pool%d" % (j + 1))
+            multiply(j, v_codes[:], v_scales[:])

@@ -16,7 +16,9 @@ ACT = mybir.ActivationFunctionType
 P = 128
 D, T, I, Q, E, U = 512, 2048, 512, 128, 512, 256
 PACK = 4
+HALF = I // 2
 PAGE_WINDOW = 544
+KS_WINDOW = 704
 FLOPS = 2 * D * Q * I + 2 * I * Q * E
 
 
@@ -32,7 +34,7 @@ def tile_attend_pagescales_kernel(tc, query, keys_words, keys_scales, kscale, vs
         key_pool = sb.tile([P, T], I32, name="key_pool")
         key_scale_pool = sb.tile([P, T], U8, name="key_scale_pool")
         q_raw = sb.tile([P, PACK, Q], F32, name="q_raw")
-        ks_pool = sb.tile([P, PAGE_WINDOW], F32, name="ks_pool")
+        ks_pool = sb.tile([P, KS_WINDOW], F32, name="ks_pool")
         vs_pool = sb.tile([P, PAGE_WINDOW], F32, name="vs_pool")
         size_col = sb.tile([P, PACK], F32, name="size_col")
         val_pool = [sb.tile([P, T], F32, name="val_pool%d" % j, tag="val_pool%d" % j, align_bytes=64) for j in range(E // P)]
@@ -43,26 +45,25 @@ def tile_attend_pagescales_kernel(tc, query, keys_words, keys_scales, kscale, vs
         nc.vector.memset(vs_pool[:, U:], 0.0)
         make_identity(nc, ident[:])
 
-        nc.sync.dma_start(token_list[:], offs)
         nc.sync.dma_start(size_col[:], size.rearrange("o (p t) -> (o p) t", t=PACK))
+        nc.sync.dma_start(page_list[:], offs2)
+        nc.sync.dma_start(ks_pool[:, :U], kscale)
+        nc.sync.dma_start(vs_pool[:, :U], vscale)
+        nc.sync.dma_start(q_raw[:], query.rearrange("(p j) q -> p j q", j=PACK))
+        nc.sync.dma_start(token_list[:], offs)
+        nc.sync.dma_start(key_pool[:], keys_words[0].rearrange("p n t -> p (n t)").bitcast(I32))
         for quad in range(4):
             nc.sync.dma_start(
                 key_scale_pool[32 * quad : 32 * quad + 4, :].bitcast(I32),
                 keys_scales[0, 4 * quad : 4 * quad + 4, :].bitcast(I32),
             )
-        nc.sync.dma_start(q_raw[:], query.rearrange("(p j) q -> p j q", j=PACK))
-        nc.sync.dma_start(key_pool[:], keys_words[0].rearrange("p n t -> p (n t)").bitcast(I32))
-        nc.sync.dma_start(page_list[:], offs2)
-        nc.sync.dma_start(vs_pool[:, :U], vscale)
-        nc.sync.dma_start(ks_pool[:, :U], kscale)
         for j in range(E // P):
             nc.sync.dma_start(val_pool[j][:], vals[j * P : (j + 1) * P, :])
 
-        def quantise(name, grouped, width, codes_tag):
-            codes = sb.tile([P, width], U32, name=name + "_codes", tag=codes_tag, align_bytes=64)
-            scales = sb.tile([P, width], U8, name=name + "_scales", align_bytes=64)
-            nc.vector.quantize_mx(out=codes[:].bitcast(FP8X4), scales=scales[:], in_=grouped[:])
-            return codes, scales
+        def quantise(name, grouped, codes):
+            scales = sb.tile(list(codes.shape), U8, name=name + "_scales", align_bytes=64)
+            nc.vector.quantize_mx(out=codes.bitcast(FP8X4), scales=scales[:], in_=grouped[:])
+            return scales
 
         def turn(rows_bf16, grouped):
             words = rows_bf16[:].bitcast(F32)
@@ -74,23 +75,10 @@ def tile_attend_pagescales_kernel(tc, query, keys_words, keys_scales, kscale, vs
                 turned[:].rearrange("p u r -> p r u"),
             )
 
-        key_scales = sb.tile([P, I], U8, name="key_scales", align_bytes=64)
-        nc.vector.tensor_copy(key_scales[:], key_scale_pool[:].indirect(token_list[:]))
-        q_grouped = sb.tile([P, PACK * Q], BF16, name="q_grouped", align_bytes=64)
-        nc.scalar.copy(q_grouped[:].rearrange("p (q j) -> p q j", j=PACK), q_raw[:].rearrange("p j q -> p q j"))
-        q_codes, q_scales = quantise("q", q_grouped, Q, "q_codes")
-        key_codes = sb.tile([P, I], U32, name="key_codes", align_bytes=64)
-        nc.vector.tensor_copy(key_codes[:], key_pool[:].bitcast(U32).indirect(token_list[:]))
+        ks_rows = sb.tile([P, I], F32, name="ks_rows")
+        nc.vector.tensor_copy(ks_rows[:], ks_pool[:].indirect(page_list[:]))
 
-        a_ps = ps.tile([P, I], F32, name="a_ps")
-        nc.tensor.matmul_mx(
-            out=a_ps[:], lhsT=q_codes[:].bitcast(FP8X4), lhsT_scale=q_scales[:],
-            rhs=key_codes[:].bitcast(FP8X4), rhs_scale=key_scales[:], start=True, stop=True,
-        )
-        a_sb = sb.tile([P, I], F32, name="a_sb")
-        nc.scalar.copy(a_sb[:], a_ps[:])
-
-        size_ps = ps.tile([P, PACK, P], F32, name="size_ps")
+        size_ps = ps.tile([P, PACK, P], F32, name="size_ps", tag="size_ps")
         for t in range(PACK):
             nc.tensor.transpose(size_ps[:, t, :], size_col[:, t : t + 1].to_broadcast([P, P]), ident[:])
         size_rows = sb.tile([P, I], F32, name="size_rows")
@@ -98,44 +86,72 @@ def tile_attend_pagescales_kernel(tc, query, keys_words, keys_scales, kscale, vs
         factor = sb.tile([P, I], F32, name="factor")
         nc.vector.tensor_tensor(factor[:], vs_pool[:].indirect(page_list[:]), size_rows[:], ALU.mult)
 
+        q_grouped = sb.tile([P, PACK * Q], BF16, name="q_grouped", align_bytes=64)
+        nc.scalar.copy(q_grouped[:].rearrange("p (q j) -> p q j", j=PACK), q_raw[:].rearrange("p j q -> p q j"))
+        q_codes = sb.tile([P, Q], U32, name="q_codes", align_bytes=64)
+        q_scales = quantise("q", q_grouped, q_codes[:])
+        key_codes = sb.tile([P, I], U32, name="key_codes", align_bytes=64)
+        nc.vector.tensor_copy(key_codes[:], key_pool[:].bitcast(U32).indirect(token_list[:]))
         s = sb.tile([P, I], F32, name="s")
-        nc.vector.tensor_tensor(s[:], ks_pool[:].indirect(page_list[:]), a_sb[:], ALU.mult)
+        scores = []
+        for h in range(2):
+            key_scales = sb.tile([P, HALF], U8, name="key_scales%d" % h, align_bytes=64)
+            nc.vector.tensor_copy(key_scales[:], key_scale_pool[:].indirect(token_list[:, h * HALF // 16 : (h + 1) * HALF // 16]))
+            a_ps = ps2.tile([P, HALF], F32, name="a_ps")
+            nc.tensor.matmul_mx(
+                out=a_ps[:], lhsT=q_codes[:].bitcast(FP8X4), lhsT_scale=q_scales[:],
+                rhs=key_codes[:, h * HALF : (h + 1) * HALF].bitcast(FP8X4), rhs_scale=key_scales[:], start=True, stop=True,
+            )
+            scores.append(a_ps)
+        for h in range(2):
+            nc.vector.tensor_tensor(s[:, h * HALF : (h + 1) * HALF], scores[h][:], ks_rows[:, h * HALF : (h + 1) * HALF], ALU.mult)
         neg_max = sb.tile([P, 1], F32, name="neg_max")
         nc.vector.tensor_reduce(neg_max[:], s[:], mybir.AxisListType.X, ALU.max, negate=True)
         prob = sb.tile([P, I], F32, name="prob")
         row_sum = sb.tile([P, 1], F32, name="row_sum")
         nc.scalar.activation(prob[:], s[:], ACT.Exp, bias=neg_max[:], scale=1.0, accum_out=row_sum[:])
 
-        def gather_values(j, grouped):
-            picked = sb.tile([P, I], BF16, name="picked%d" % j, align_bytes=64)
-            nc.vector.tensor_copy(picked[:], val_pool[j][:].indirect(token_list[:]))
+        def gather_values(j, grouped, tag):
+            picked = sb.tile([P, I], BF16, name="picked%d" % j, tag=tag, align_bytes=64)
+            if j == 0:
+                rounded = sb.tile([P, T], BF16, name="rounded")
+                nc.scalar.copy(rounded[:], val_pool[j][:])
+                nc.scalar.activation(picked[:], rounded[:].indirect(token_list[:]), ACT.Copy)
+            else:
+                nc.vector.tensor_copy(picked[:], val_pool[j][:].indirect(token_list[:]))
             turn(picked, grouped)
 
-        def multiply(j, v_codes, v_scales):
-            o_ps = ps2.tile([P, P], F32, name="o_ps")
+        def multiply(j, width, v_codes, v_scales, copy):
+            o_ps = ps.tile([P, width], F32, name="o_ps%d" % j)
             nc.tensor.matmul_mx(
-                out=o_ps[:], lhsT=first_codes[:, :Q].bitcast(FP8X4), lhsT_scale=first_scales[:, :Q],
+                out=o_ps[:], lhsT=codes[:, :Q].bitcast(FP8X4), lhsT_scale=first_scales[:, :Q],
                 rhs=v_codes.bitcast(FP8X4), rhs_scale=v_scales, start=True, stop=True,
             )
-            o_sb = sb.tile([P, P], F32, name="o_sb%d" % j)
-            nc.scalar.copy(o_sb[:], o_ps[:])
-            nc.sync.dma_start(out[:, j * P : (j + 1) * P], o_sb[:])
+            o_sb = sb.tile([P, width], F32, name="o_sb%d" % j)
+            copy(o_sb[:], o_ps[:])
+            nc.sync.dma_start(out[:, j * P : j * P + width], o_sb[:])
 
         first_grouped = sb.tile([P, PACK * (Q + P)], BF16, name="first_grouped", align_bytes=64)
-        gather_values(0, first_grouped[:, PACK * Q :])
+        middle_grouped = sb.tile([P, PACK * 2 * P], BF16, name="middle_grouped", align_bytes=64)
+        last_grouped = sb.tile([P, PACK * P], BF16, name="last_grouped", align_bytes=64)
+        gather_values(0, first_grouped[:, PACK * Q :], "picked0")
 
         inv_sum = sb.tile([P, 1], F32, name="inv_sum")
         nc.vector.reciprocal(inv_sum[:], row_sum[:])
+        weighted = sb.tile([P, I], F32, name="weighted")
+        nc.vector.tensor_tensor(weighted[:], prob[:], factor[:], ALU.mult)
         w = sb.tile([P, I], BF16, name="w", align_bytes=64)
-        nc.vector.scalar_tensor_tensor(w[:], prob[:], inv_sum[:], factor[:], ALU.mult, ALU.mult)
+        nc.scalar.activation(w[:], weighted[:], ACT.Copy, scale=inv_sum[:])
         turn(w, first_grouped[:, : PACK * Q])
 
-        grouped = [sb.tile([P, PACK * P], BF16, name="grouped%d" % j, align_bytes=64) for j in range(1, E // P)]
-        gather_values(1, grouped[0][:])
-        first_codes, first_scales = quantise("first", first_grouped, Q + P, "val_pool1")
-        multiply(0, first_codes[:, Q:], first_scales[:, Q:])
-        for j in range(1, E // P):
-            if j + 1 < E // P:
-                gather_values(j + 1, grouped[j][:])
-            v_codes, v_scales = quantise("v%d" % j, grouped[j - 1], P, "val_pool%d" % (j + 1))
-            multiply(j, v_codes[:], v_scales[:])
+        gather_values(1, middle_grouped[:, : PACK * P], "picked1")
+        gather_values(2, middle_grouped[:, PACK * P :], "picked2")
+        gather_values(3, last_grouped[:], "picked3")
+        codes = sb.tile([P, Q + 3 * P], U32, name="codes", tag="val_pool3", align_bytes=64)
+        first_scales = quantise("first", first_grouped, codes[:, : Q + P])
+        middle_scales = quantise("middle", middle_grouped, codes[:, Q + P :])
+        last_codes = sb.tile([P, P], U32, name="last_codes", align_bytes=64)
+        last_scales = quantise("last", last_grouped, last_codes[:])
+        multiply(0, P, codes[:, Q : Q + P], first_scales[:, Q:], nc.scalar.copy)
+        multiply(1, 2 * P, codes[:, Q + P :], middle_scales[:], nc.scalar.copy)
+        multiply(3, P, last_codes[:], last_scales[:], nc.vector.tensor_copy)

@@ -16,9 +16,12 @@ ACT = mybir.ActivationFunctionType
 P = 128
 D, T, I, Q, E, U = 512, 2048, 512, 128, 512, 256
 PACK = 4
+GROUP = 16
 HALF = I // 2
-PAGE_WINDOW = 544
-KS_WINDOW = 704
+KSCALE_COLUMNS = 704
+VSCALE_COLUMNS = 544
+SCALAR_BLOCK = 0
+LAST_BLOCK = E // P - 1
 FLOPS = 2 * D * Q * I + 2 * I * Q * E
 
 
@@ -29,13 +32,13 @@ def tile_attend_pagescales_kernel(tc, query, keys_words, keys_scales, kscale, vs
         ps = ctx.enter_context(tc.psum_pool(name="ps", bufs=1))
         ps2 = ctx.enter_context(tc.psum_pool(name="ps2", bufs=2))
 
-        token_list = sb.tile([P, I // 16], U16, name="token_list")
-        page_list = sb.tile([P, I // 16], U16, name="page_list")
+        token_list = sb.tile([P, I // GROUP], U16, name="token_list")
+        page_list = sb.tile([P, I // GROUP], U16, name="page_list")
         key_pool = sb.tile([P, T], I32, name="key_pool")
         key_scale_pool = sb.tile([P, T], U8, name="key_scale_pool")
         q_raw = sb.tile([P, PACK, Q], F32, name="q_raw")
-        ks_pool = sb.tile([P, KS_WINDOW], F32, name="ks_pool")
-        vs_pool = sb.tile([P, PAGE_WINDOW], F32, name="vs_pool")
+        ks_pool = sb.tile([P, KSCALE_COLUMNS], F32, name="ks_pool")
+        vs_pool = sb.tile([P, VSCALE_COLUMNS], F32, name="vs_pool")
         size_col = sb.tile([P, PACK], F32, name="size_col")
         val_pool = [sb.tile([P, T], F32, name="val_pool%d" % j, tag="val_pool%d" % j, align_bytes=64) for j in range(E // P)]
         ident = sb.tile([P, P], F32, name="ident")
@@ -45,18 +48,15 @@ def tile_attend_pagescales_kernel(tc, query, keys_words, keys_scales, kscale, vs
         nc.vector.memset(vs_pool[:, U:], 0.0)
         make_identity(nc, ident[:])
 
+        nc.sync.dma_start(ks_pool[:, :U], kscale)
         nc.sync.dma_start(size_col[:], size.rearrange("o (p t) -> (o p) t", t=PACK))
         nc.sync.dma_start(page_list[:], offs2)
-        nc.sync.dma_start(ks_pool[:, :U], kscale)
         nc.sync.dma_start(vs_pool[:, :U], vscale)
-        nc.sync.dma_start(q_raw[:], query.rearrange("(p j) q -> p j q", j=PACK))
+        nc.sync.dma_start(q_raw[:], query.rearrange("(p t) q -> p t q", t=PACK))
         nc.sync.dma_start(token_list[:], offs)
         nc.sync.dma_start(key_pool[:], keys_words[0].rearrange("p n t -> p (n t)").bitcast(I32))
-        for quad in range(4):
-            nc.sync.dma_start(
-                key_scale_pool[32 * quad : 32 * quad + 4, :].bitcast(I32),
-                keys_scales[0, 4 * quad : 4 * quad + 4, :].bitcast(I32),
-            )
+        for r in range(4):
+            nc.sync.dma_start(key_scale_pool[r:P:32, :].bitcast(I32), keys_scales[0, r:16:4, :].bitcast(I32))
         for j in range(E // P):
             nc.sync.dma_start(val_pool[j][:], vals[j * P : (j + 1) * P, :])
 
@@ -66,19 +66,19 @@ def tile_attend_pagescales_kernel(tc, query, keys_words, keys_scales, kscale, vs
             return scales
 
         def turn(rows_bf16, grouped):
-            words = rows_bf16[:].bitcast(F32)
+            pairs = rows_bf16[:].bitcast(F32)
             turned = ps2.tile([P, 2, P], F32, name="turned")
-            for u in range(2):
-                nc.tensor.transpose(turned[:, u, :], words[:, u : I // 2 : 2], ident[:])
+            for n in range(2):
+                nc.tensor.transpose(turned[:, n, :], pairs[:, n : I // 2 : 2], ident[:])
             nc.scalar.copy(
-                grouped.bitcast(F32).rearrange("p (r u) -> p r u", u=2),
-                turned[:].rearrange("p u r -> p r u"),
+                grouped.bitcast(F32).rearrange("p (c n) -> p c n", n=2),
+                turned[:].rearrange("p n c -> p c n"),
             )
 
         ks_rows = sb.tile([P, I], F32, name="ks_rows")
         nc.vector.tensor_copy(ks_rows[:], ks_pool[:].indirect(page_list[:]))
 
-        size_ps = ps.tile([P, PACK, P], F32, name="size_ps", tag="size_ps")
+        size_ps = ps.tile([P, PACK, P], F32, name="size_ps")
         for t in range(PACK):
             nc.tensor.transpose(size_ps[:, t, :], size_col[:, t : t + 1].to_broadcast([P, P]), ident[:])
         size_rows = sb.tile([P, I], F32, name="size_rows")
@@ -87,33 +87,36 @@ def tile_attend_pagescales_kernel(tc, query, keys_words, keys_scales, kscale, vs
         nc.vector.tensor_tensor(factor[:], vs_pool[:].indirect(page_list[:]), size_rows[:], ALU.mult)
 
         q_grouped = sb.tile([P, PACK * Q], BF16, name="q_grouped", align_bytes=64)
-        nc.scalar.copy(q_grouped[:].rearrange("p (q j) -> p q j", j=PACK), q_raw[:].rearrange("p j q -> p q j"))
+        nc.scalar.copy(q_grouped[:].rearrange("p (q t) -> p q t", t=PACK), q_raw[:].rearrange("p t q -> p q t"))
         q_codes = sb.tile([P, Q], U32, name="q_codes", align_bytes=64)
         q_scales = quantise("q", q_grouped, q_codes[:])
+
         key_codes = sb.tile([P, I], U32, name="key_codes", align_bytes=64)
         nc.vector.tensor_copy(key_codes[:], key_pool[:].bitcast(U32).indirect(token_list[:]))
         s = sb.tile([P, I], F32, name="s")
-        scores = []
+        a_halves = []
         for h in range(2):
             key_scales = sb.tile([P, HALF], U8, name="key_scales%d" % h, align_bytes=64)
-            nc.vector.tensor_copy(key_scales[:], key_scale_pool[:].indirect(token_list[:, h * HALF // 16 : (h + 1) * HALF // 16]))
+            half_list = token_list[:, h * HALF // GROUP : (h + 1) * HALF // GROUP]
+            nc.vector.tensor_copy(key_scales[:], key_scale_pool[:].indirect(half_list))
             a_ps = ps2.tile([P, HALF], F32, name="a_ps")
             nc.tensor.matmul_mx(
                 out=a_ps[:], lhsT=q_codes[:].bitcast(FP8X4), lhsT_scale=q_scales[:],
                 rhs=key_codes[:, h * HALF : (h + 1) * HALF].bitcast(FP8X4), rhs_scale=key_scales[:], start=True, stop=True,
             )
-            scores.append(a_ps)
+            a_halves.append(a_ps)
         for h in range(2):
-            nc.vector.tensor_tensor(s[:, h * HALF : (h + 1) * HALF], scores[h][:], ks_rows[:, h * HALF : (h + 1) * HALF], ALU.mult)
+            nc.vector.tensor_tensor(s[:, h * HALF : (h + 1) * HALF], a_halves[h][:], ks_rows[:, h * HALF : (h + 1) * HALF], ALU.mult)
+
         neg_max = sb.tile([P, 1], F32, name="neg_max")
         nc.vector.tensor_reduce(neg_max[:], s[:], mybir.AxisListType.X, ALU.max, negate=True)
         prob = sb.tile([P, I], F32, name="prob")
         row_sum = sb.tile([P, 1], F32, name="row_sum")
         nc.scalar.activation(prob[:], s[:], ACT.Exp, bias=neg_max[:], scale=1.0, accum_out=row_sum[:])
 
-        def gather_values(j, grouped, tag):
-            picked = sb.tile([P, I], BF16, name="picked%d" % j, tag=tag, align_bytes=64)
-            if j == 0:
+        def gather_values(j, grouped):
+            picked = sb.tile([P, I], BF16, name="picked%d" % j, align_bytes=64)
+            if j == SCALAR_BLOCK:
                 rounded = sb.tile([P, T], BF16, name="rounded")
                 nc.scalar.copy(rounded[:], val_pool[j][:])
                 nc.scalar.activation(picked[:], rounded[:].indirect(token_list[:]), ACT.Copy)
@@ -134,7 +137,7 @@ def tile_attend_pagescales_kernel(tc, query, keys_words, keys_scales, kscale, vs
         first_grouped = sb.tile([P, PACK * (Q + P)], BF16, name="first_grouped", align_bytes=64)
         middle_grouped = sb.tile([P, PACK * 2 * P], BF16, name="middle_grouped", align_bytes=64)
         last_grouped = sb.tile([P, PACK * P], BF16, name="last_grouped", align_bytes=64)
-        gather_values(0, first_grouped[:, PACK * Q :], "picked0")
+        gather_values(0, first_grouped[:, PACK * Q :])
 
         inv_sum = sb.tile([P, 1], F32, name="inv_sum")
         nc.vector.reciprocal(inv_sum[:], row_sum[:])
@@ -144,14 +147,16 @@ def tile_attend_pagescales_kernel(tc, query, keys_words, keys_scales, kscale, vs
         nc.scalar.activation(w[:], weighted[:], ACT.Copy, scale=inv_sum[:])
         turn(w, first_grouped[:, : PACK * Q])
 
-        gather_values(1, middle_grouped[:, : PACK * P], "picked1")
-        gather_values(2, middle_grouped[:, PACK * P :], "picked2")
-        gather_values(3, last_grouped[:], "picked3")
-        codes = sb.tile([P, Q + 3 * P], U32, name="codes", tag="val_pool3", align_bytes=64)
+        gather_values(1, middle_grouped[:, : PACK * P])
+        gather_values(2, middle_grouped[:, PACK * P :])
+        gather_values(LAST_BLOCK, last_grouped[:])
+
+        codes = sb.tile([P, Q + LAST_BLOCK * P], U32, name="codes", tag="val_pool%d" % LAST_BLOCK, align_bytes=64)
         first_scales = quantise("first", first_grouped, codes[:, : Q + P])
         middle_scales = quantise("middle", middle_grouped, codes[:, Q + P :])
         last_codes = sb.tile([P, P], U32, name="last_codes", align_bytes=64)
         last_scales = quantise("last", last_grouped, last_codes[:])
+
         multiply(0, P, codes[:, Q : Q + P], first_scales[:, Q:], nc.scalar.copy)
         multiply(1, 2 * P, codes[:, Q + P :], middle_scales[:], nc.scalar.copy)
-        multiply(3, P, last_codes[:], last_scales[:], nc.vector.tensor_copy)
+        multiply(LAST_BLOCK, P, last_codes[:], last_scales[:], nc.vector.tensor_copy)

from contextlib import ExitStack

import concourse.mybir as mybir
from concourse.masks import make_identity

F32 = mybir.dt.float32
BF16 = mybir.dt.bfloat16
I32 = mybir.dt.int32
U32 = mybir.dt.uint32
U16 = mybir.dt.uint16
U8 = mybir.dt.uint8
FP8X4 = mybir.dt.float8_e4m3fn_x4
ALU = mybir.AluOpType
ACT = mybir.ActivationFunctionType

P = 128
D, T, I, Q, E, U = 512, 2048, 512, 128, 512, 256
PACK = 4
GROUP = 16
HALF = I // 2
KSCALE_COLUMNS = 704
VSCALE_COLUMNS = 544
SCALAR_BLOCK = 0
LAST_BLOCK = E // P - 1
FLOPS = 2 * D * Q * I + 2 * I * Q * E


def tile_attend_pagescales_kernel(tc, query, keys_words, keys_scales, kscale, vscale, size, vals, offs, offs2, out):
    nc = tc.nc
    with ExitStack() as ctx:
        sb = ctx.enter_context(tc.tile_pool(name="sb", bufs=1))
        ps = ctx.enter_context(tc.psum_pool(name="ps", bufs=1))
        ps2 = ctx.enter_context(tc.psum_pool(name="ps2", bufs=2))

        token_list = sb.tile([P, I // GROUP], U16, name="token_list")
        page_list = sb.tile([P, I // GROUP], U16, name="page_list")
        key_pool = sb.tile([P, T], I32, name="key_pool")
        key_scale_pool = sb.tile([P, T], U8, name="key_scale_pool")
        q_raw = sb.tile([P, PACK, Q], F32, name="q_raw")
        ks_pool = sb.tile([P, KSCALE_COLUMNS], F32, name="ks_pool")
        vs_pool = sb.tile([P, VSCALE_COLUMNS], F32, name="vs_pool")
        size_col = sb.tile([P, PACK], F32, name="size_col")
        val_pool = [sb.tile([P, T], F32, name="val_pool%d" % j, tag="val_pool%d" % j, align_bytes=64) for j in range(E // P)]
        ident = sb.tile([P, P], F32, name="ident")

        nc.gpsimd.memset(key_scale_pool[:].bitcast(I32), 0)
        nc.vector.memset(ks_pool[:, U:], 0.0)
        nc.vector.memset(vs_pool[:, U:], 0.0)
        make_identity(nc, ident[:])

        nc.sync.dma_start(ks_pool[:, :U], kscale)
        nc.sync.dma_start(size_col[:], size.rearrange("o (p t) -> (o p) t", t=PACK))
        nc.sync.dma_start(page_list[:], offs2)
        nc.sync.dma_start(vs_pool[:, :U], vscale)
        nc.sync.dma_start(q_raw[:], query.rearrange("(p t) q -> p t q", t=PACK))
        nc.sync.dma_start(token_list[:], offs)
        nc.sync.dma_start(key_pool[:], keys_words[0].rearrange("p n t -> p (n t)").bitcast(I32))
        for r in range(4):
            nc.sync.dma_start(key_scale_pool[r:P:32, :].bitcast(I32), keys_scales[0, r:16:4, :].bitcast(I32))
        for j in range(E // P):
            nc.sync.dma_start(val_pool[j][:], vals[j * P : (j + 1) * P, :])

        def quantise(name, grouped, codes):
            scales = sb.tile(list(codes.shape), U8, name=name + "_scales", align_bytes=64)
            nc.vector.quantize_mx(out=codes.bitcast(FP8X4), scales=scales[:], in_=grouped[:])
            return scales

        def turn(rows_bf16, grouped):
            pairs = rows_bf16[:].bitcast(F32)
            turned = ps2.tile([P, 2, P], F32, name="turned")
            for n in range(2):
                nc.tensor.transpose(turned[:, n, :], pairs[:, n : I // 2 : 2], ident[:])
            nc.scalar.copy(
                grouped.bitcast(F32).rearrange("p (c n) -> p c n", n=2),
                turned[:].rearrange("p n c -> p c n"),
            )

        ks_rows = sb.tile([P, I], F32, name="ks_rows")
        nc.vector.tensor_copy(ks_rows[:], ks_pool[:].indirect(page_list[:]))

        size_ps = ps.tile([P, PACK, P], F32, name="size_ps")
        for t in range(PACK):
            nc.tensor.transpose(size_ps[:, t, :], size_col[:, t : t + 1].to_broadcast([P, P]), ident[:])
        size_rows = sb.tile([P, I], F32, name="size_rows")
        nc.scalar.copy(size_rows[:].rearrange("q (p t) -> q p t", t=PACK), size_ps[:].rearrange("q t p -> q p t"))
        factor = sb.tile([P, I], F32, name="factor")
        nc.vector.tensor_tensor(factor[:], vs_pool[:].indirect(page_list[:]), size_rows[:], ALU.mult)

        q_grouped = sb.tile([P, PACK * Q], BF16, name="q_grouped", align_bytes=64)
        nc.scalar.copy(q_grouped[:].rearrange("p (q t) -> p q t", t=PACK), q_raw[:].rearrange("p t q -> p q t"))
        q_codes = sb.tile([P, Q], U32, name="q_codes", align_bytes=64)
        q_scales = quantise("q", q_grouped, q_codes[:])

        key_codes = sb.tile([P, I], U32, name="key_codes", align_bytes=64)
        nc.vector.tensor_copy(key_codes[:], key_pool[:].bitcast(U32).indirect(token_list[:]))
        s = sb.tile([P, I], F32, name="s")
        a_halves = []
        for h in range(2):
            key_scales = sb.tile([P, HALF], U8, name="key_scales%d" % h, align_bytes=64)
            half_list = token_list[:, h * HALF // GROUP : (h + 1) * HALF // GROUP]
            nc.vector.tensor_copy(key_scales[:], key_scale_pool[:].indirect(half_list))
            a_ps = ps2.tile([P, HALF], F32, name="a_ps")
            nc.tensor.matmul_mx(
                out=a_ps[:], lhsT=q_codes[:].bitcast(FP8X4), lhsT_scale=q_scales[:],
                rhs=key_codes[:, h * HALF : (h + 1) * HALF].bitcast(FP8X4), rhs_scale=key_scales[:], start=True, stop=True,
            )
            a_halves.append(a_ps)
        for h in range(2):
            nc.vector.tensor_tensor(s[:, h * HALF : (h + 1) * HALF], a_halves[h][:], ks_rows[:, h * HALF : (h + 1) * HALF], ALU.mult)

        neg_max = sb.tile([P, 1], F32, name="neg_max")
        nc.vector.tensor_reduce(neg_max[:], s[:], mybir.AxisListType.X, ALU.max, negate=True)
        prob = sb.tile([P, I], F32, name="prob")
        row_sum = sb.tile([P, 1], F32, name="row_sum")
        nc.scalar.activation(prob[:], s[:], ACT.Exp, bias=neg_max[:], scale=1.0, accum_out=row_sum[:])

        def gather_values(j, grouped):
            picked = sb.tile([P, I], BF16, name="picked%d" % j, align_bytes=64)
            if j == SCALAR_BLOCK:
                rounded = sb.tile([P, T], BF16, name="rounded")
                nc.scalar.copy(rounded[:], val_pool[j][:])
                nc.scalar.activation(picked[:], rounded[:].indirect(token_list[:]), ACT.Copy)
            else:
                nc.vector.tensor_copy(picked[:], val_pool[j][:].indirect(token_list[:]))
            turn(picked, grouped)

        def multiply(j, width, v_codes, v_scales, copy):
            o_ps = ps.tile([P, width], F32, name="o_ps%d" % j)
            nc.tensor.matmul_mx(
                out=o_ps[:], lhsT=codes[:, :Q].bitcast(FP8X4), lhsT_scale=first_scales[:, :Q],
                rhs=v_codes.bitcast(FP8X4), rhs_scale=v_scales, start=True, stop=True,
            )
            o_sb = sb.tile([P, width], F32, name="o_sb%d" % j)
            copy(o_sb[:], o_ps[:])
            nc.sync.dma_start(out[:, j * P : j * P + width], o_sb[:])

        first_grouped = sb.tile([P, PACK * (Q + P)], BF16, name="first_grouped", align_bytes=64)
        middle_grouped = sb.tile([P, PACK * 2 * P], BF16, name="middle_grouped", align_bytes=64)
        last_grouped = sb.tile([P, PACK * P], BF16, name="last_grouped", align_bytes=64)
        gather_values(0, first_grouped[:, PACK * Q :])

        inv_sum = sb.tile([P, 1], F32, name="inv_sum")
        nc.vector.reciprocal(inv_sum[:], row_sum[:])
        weighted = sb.tile([P, I], F32, name="weighted")
        nc.vector.tensor_tensor(weighted[:], prob[:], factor[:], ALU.mult)
        w = sb.tile([P, I], BF16, name="w", align_bytes=64)
        nc.scalar.activation(w[:], weighted[:], ACT.Copy, scale=inv_sum[:])
        turn(w, first_grouped[:, : PACK * Q])

        gather_values(1, middle_grouped[:, : PACK * P])
        gather_values(2, middle_grouped[:, PACK * P :])
        gather_values(LAST_BLOCK, last_grouped[:])

        codes = sb.tile([P, Q + LAST_BLOCK * P], U32, name="codes", tag="val_pool%d" % LAST_BLOCK, align_bytes=64)
        first_scales = quantise("first", first_grouped, codes[:, : Q + P])
        middle_scales = quantise("middle", middle_grouped, codes[:, Q + P :])
        last_codes = sb.tile([P, P], U32, name="last_codes", align_bytes=64)
        last_scales = quantise("last", last_grouped, last_codes[:])

        multiply(0, P, codes[:, Q : Q + P], first_scales[:, Q:], nc.scalar.copy)
        multiply(1, 2 * P, codes[:, Q + P :], middle_scales[:], nc.scalar.copy)
        multiply(LAST_BLOCK, P, last_codes[:], last_scales[:], nc.vector.tensor_copy)
